import numpy as np
import ml_dtypes


def mxq(x, axis, fmt="e4m3"):
    dtype, down = {"e4m3": (ml_dtypes.float8_e4m3fn, 7), "e5m2": (ml_dtypes.float8_e5m2, 14)}[fmt]
    v = np.moveaxis(np.asarray(x, np.float32).astype(ml_dtypes.bfloat16).astype(np.float64), axis, -1)
    blocks = v.reshape(v.shape[:-1] + (-1, 32))
    amax = np.abs(blocks).max(-1, keepdims=True)
    byte = np.maximum(np.where(amax > 0, np.frexp(amax)[1] - 1 + 127, 0) - down, 1)
    scale = np.exp2(byte - 127.0)
    codes = (blocks / scale).astype(np.float32).astype(dtype).astype(np.float64)
    return np.moveaxis((codes * scale).reshape(v.shape), -1, axis)


WIDE = False


def mx_kscale(k):
    if not WIDE:
        return np.ones(k)
    levels = np.array([10, -10, 5, -5, 0])
    if k % 512:
        return np.exp2(np.random.permutation(np.resize(levels, k // 32))).repeat(32)
    a = np.empty((k // 512, 16))
    for p in range(k // 512):
        a[p, :8] = np.random.permutation(np.resize(levels, 8))
        for g in range(8):
            far = levels[np.abs(levels - a[p, g]) >= 10]
            a[p, g + 8] = far[np.random.randint(len(far))]
    return np.exp2(a.ravel()).repeat(32)


def f64(x):
    return np.asarray(x).astype(np.float64)


def striped(idx):
    return np.tile(idx.reshape(-1, 16).T, (8, 1)).astype(np.uint16)


def unstriped(offs):
    return offs[:16].T.reshape(-1).astype(np.int64)


def pack_weight(w):
    k, n = w.shape
    w = f64(np.asarray(w, np.float32).astype(ml_dtypes.bfloat16)).reshape(k // 32, 32, n)
    amax = np.abs(w).max(1)
    byte = np.clip(np.where(amax > 0, np.frexp(amax)[1] - 1 + 127 - 7, 1), 1, 254)
    scaled = (w * np.exp2(127.0 - byte)[:, None, :]).reshape(k, n).astype(np.float32)
    words = np.ascontiguousarray(scaled.reshape(k // 512, 128, 4, n).transpose(0, 1, 3, 2)).astype(ml_dtypes.float8_e4m3fn).view(np.uint8)
    return words, np.ascontiguousarray(byte.astype(np.uint8).reshape(k // 512, 16, n))


def unpack_weight(words, scales):
    g, p, n, _ = words.shape
    vals = np.ascontiguousarray(words).view(ml_dtypes.float8_e4m3fn).astype(np.float64) * np.repeat(np.exp2(scales.astype(np.float64) - 127.0), 8, axis=1)[..., None]
    return vals.transpose(0, 1, 3, 2).reshape(g * 512, n)


def planes(y):
    n, m = y.shape
    v = y.astype(np.float32).astype(ml_dtypes.bfloat16).astype(np.float64).reshape(n // 32, 32, m)
    top = np.abs(v).max(1)
    byte = np.clip(np.where(top > 0, np.frexp(top)[1] - 1 + 127 - 7, 1), 1, 254)
    codes = (v * np.exp2(127.0 - byte)[:, None, :]).reshape(n, m).astype(np.float32).astype(ml_dtypes.float8_e4m3fn).view(np.uint8)
    words = codes.reshape(n // 512, 128, 4, m).transpose(0, 1, 3, 2)
    return np.ascontiguousarray(words), np.ascontiguousarray(byte.astype(np.uint8).reshape(n // 512, 16, m))


def silu(v):
    return v / (1.0 + np.exp(-np.maximum(v, -700.0)))


K, T, S, W, H, N = 1024, 2048, 512, 1024, 512, 512


def setup_inputs():
    n = np.random.standard_normal
    s = mx_kscale(K)[:, None]
    u = mx_kscale(H)
    packed_xT = pack_weight(n((K, T)) * s)
    packed_eT = pack_weight(n((K, W)) * s)
    return {
        "x_words": packed_xT[0],
        "x_scales": packed_xT[1],
        "e_words": packed_eT[0],
        "e_scales": packed_eT[1],
        "w1": (n((K, H)) / np.sqrt(2 * K) / s * u).astype(np.float32),
        "w2": (n((K, H)) / np.sqrt(2 * K) / s * u).astype(np.float32),
        "w3": (n((H, N)) / np.sqrt(H) / u[:, None]).astype(np.float32),
        "skip": (n((N, S))).astype(np.float32),
        "offs": striped(np.random.permutation(T)[:S]),
        "tok": striped(np.random.permutation(W)[:S]),
    }


def reference(x_words, x_scales, e_words, e_scales, w1, w2, w3, skip, offs, tok):
    xq = unpack_weight(x_words, x_scales)[:, unstriped(offs)]
    e_tok = unpack_weight(e_words, e_scales)[:, unstriped(tok)]
    h = silu(mxq(f64(w1), 0, "e4m3").T @ xq + mxq(f64(w2), 0, "e4m3").T @ e_tok)
    y = mxq(f64(w3), 0, "e4m3").T @ mxq(h, 0, "e4m3")
    out_0 = y + f64(skip)
    return (out_0,) + planes(out_0)

@@ -1,0 +1,276 @@
+from contextlib import ExitStack
+
+import concourse.mybir as mybir
+
+F32 = mybir.dt.float32
+BF16 = mybir.dt.bfloat16
+I32 = mybir.dt.int32
+U32 = mybir.dt.uint32
+U16 = mybir.dt.uint16
+U8 = mybir.dt.uint8
+FP8X4 = mybir.dt.float8_e4m3fn_x4
+SILU = mybir.ActivationFunctionType.Silu
+ADD = mybir.AluOpType.add
+
+K, T, S, W, H, N = 1024, 2048, 512, 1024, 512, 512
+FLOPS = 2 * (2 * K * H * S + H * N * S)
+
+P = 128
+PACK = 4
+K_PASS = P * PACK
+HALF = S // 2
+QUARTER = S // 4
+OFFSETS_PER_COLUMN = 16
+QUADRANT = 32
+SCALE_ROWS = 4
+X_SCALE_ROW = 0
+E_SCALE_ROW = 8
+
+
+def tile_picked_zeagle_silu_po_kernel(
+    tc, x_words, x_scales, e_words, e_scales, w1, w2, w3, skip, offs, tok, out_0, out_1, out_2
+):
+    nc = tc.nc
+    with ExitStack() as ctx:
+        keep = ctx.enter_context(tc.tile_pool(name="keep", bufs=1))
+        psum = ctx.enter_context(tc.psum_pool(name="psum", bufs=1))
+
+        def load_weight(name, rows):
+            raw = keep.tile([P, PACK, rows.shape[1]], F32, name=name + "_raw")
+            nc.sync.dma_start(out=raw[:], in_=rows.rearrange("(p j) c -> p j c", j=PACK))
+            return raw
+
+        def load_words(name, words):
+            table = keep.tile([P, words.shape[1]], I32, name=name + "_table", align_bytes=64)
+            nc.sync.dma_start(out=table[:], in_=words.rearrange("p c r -> p (c r)").bitcast(I32))
+            return table
+
+        def clear_scales(name, scales):
+            table = keep.tile([P, scales.shape[2]], U8, name=name + "_scale_table", align_bytes=64)
+            nc.vector.memset(table[:].bitcast(I32), 0)
+            return table
+
+        def load_scales(table, scales, first_row, quadrants):
+            for q in quadrants:
+                top = QUADRANT * q + first_row
+                nc.sync.dma_start(
+                    out=table[top : top + 2 * SCALE_ROWS, :].bitcast(I32),
+                    in_=scales[:, SCALE_ROWS * q : SCALE_ROWS * (q + 1), :].bitcast(I32),
+                )
+
+        def round_weight(name, raw):
+            src = raw[:].rearrange("p j (m u e) -> p u m j e", u=2, e=2)
+            pairs = []
+            for u in range(2):
+                grouped = keep.tile([P, 2, P, PACK], BF16, name=f"{name}_bf{u}", align_bytes=64)
+                dst = grouped[:].rearrange("p e m j -> p m j e")
+                if u == 0:
+                    nc.vector.tensor_copy(out=dst, in_=src[:, u])
+                else:
+                    nc.scalar.copy(out=dst, in_=src[:, u])
+                pairs.append(grouped)
+            return pairs
+
+        def quantize(name, values, width):
+            codes = keep.tile([P, width], U32, name=name + "_codes", align_bytes=64)
+            scales = keep.tile([P, width], U8, name=name + "_scales", align_bytes=64)
+            nc.vector.quantize_mx(out=codes[:].bitcast(FP8X4), scales=scales[:], in_=values)
+            return codes, scales
+
+        def quantize_weight(name, pairs):
+            made = [
+                quantize(f"{name}_q{u}", pairs[u][:].rearrange("p e m j -> p (e m j)"), 2 * P) for u in range(2)
+            ]
+            return [
+                (made[t // 2][0][:, (t % 2) * P : (t % 2 + 1) * P], made[t // 2][1][:, (t % 2) * P : (t % 2 + 1) * P])
+                for t in range(PACK)
+            ]
+
+        def gather_words(name, table, offsets, count):
+            picked = keep.tile([P, count], U32, name=name + "_picked", align_bytes=64)
+            nc.vector.tensor_copy(out=picked[:], in_=table[:].bitcast(U32).indirect(offsets))
+            return picked
+
+        def gather_scales(name, table, offsets):
+            picked = keep.tile([P, S], U8, name=name + "_picked_scales", align_bytes=64)
+            nc.vector.tensor_copy(out=picked[:], in_=table[:].indirect(offsets))
+            return picked
+
+        plane_banks = [psum.tile([P, S], F32, name=f"bank{t}") for t in range(PACK)]
+        side_banks = [psum.tile([P, S], F32, name=f"bank{PACK + c}") for c in range(2)]
+
+        def hidden_matmul(out, weight, words, scales, scale_row, cols, start, stop):
+            nc.tensor.matmul_mx(
+                out=out,
+                lhsT=weight[0].bitcast(FP8X4),
+                lhsT_scale=weight[1],
+                rhs=words.bitcast(FP8X4),
+                rhs_scale=scales[scale_row:, cols],
+                start=start,
+                stop=stop,
+            )
+
+        def early_pass(weight, words, scales, scale_row, start):
+            for t in range(PACK):
+                hidden_matmul(plane_banks[t][:, :HALF], weight[t], words[:, :HALF], scales, scale_row, slice(0, HALF), start, False)
+            for c in range(2):
+                cols = slice(HALF + c * QUARTER, HALF + (c + 1) * QUARTER)
+                hidden_matmul(side_banks[c][:, :QUARTER], weight[0], words[:, cols], scales, scale_row, cols, start, False)
+
+        x_scale_table = clear_scales("x", x_scales)
+        e_scale_table = clear_scales("e", e_scales)
+        w1_raw0 = load_weight("w1_0", w1[:K_PASS, :])
+        offs_list = keep.tile([P, S // OFFSETS_PER_COLUMN], U16, name="offs_list")
+        nc.sync.dma_start(offs_list[:], offs)
+        load_scales(x_scale_table, x_scales, X_SCALE_ROW, (0, 1))
+        x_table0 = load_words("x0", x_words[0])
+        load_scales(x_scale_table, x_scales, X_SCALE_ROW, (2, 3))
+        w1_raw1 = load_weight("w1_1", w1[K_PASS:, :])
+        tok_list = keep.tile([P, S // OFFSETS_PER_COLUMN], U16, name="tok_list")
+        nc.sync.dma_start(tok_list[:], tok)
+        load_scales(e_scale_table, e_scales, E_SCALE_ROW, (0, 1))
+        x_table1 = load_words("x1", x_words[1])
+        load_scales(e_scale_table, e_scales, E_SCALE_ROW, (2, 3))
+        w2_raw0 = load_weight("w2_0", w2[:K_PASS, :])
+        e_table0 = load_words("e0", e_words[0])
+        w2_raw1 = load_weight("w2_1", w2[K_PASS:, :])
+        e_table1 = load_words("e1", e_words[1])
+        w3_raw = [load_weight(f"w3_{half}", w3[:, half * HALF : (half + 1) * HALF]) for half in range(2)]
+        skip_rows = [load_weight(f"skip_{half}", skip[:, half * HALF : (half + 1) * HALF]) for half in range(2)]
+
+        w1_q0 = quantize_weight("w1_0", round_weight("w1_0", w1_raw0))
+        x_picked_scales = gather_scales("x", x_scale_table, offs_list[:])
+        x_picked0 = gather_words("x0", x_table0, offs_list[:], S)
+        early_pass(w1_q0, x_picked0, x_picked_scales, X_SCALE_ROW, True)
+        w1_q1 = quantize_weight("w1_1", round_weight("w1_1", w1_raw1))
+        x_picked1 = gather_words("x1", x_table1, offs_list[:], S)
+        early_pass(w1_q1, x_picked1, x_picked_scales, X_SCALE_ROW + SCALE_ROWS, False)
+        e_picked_scales = gather_scales("e", e_scale_table, tok_list[:])
+        w2_q0 = quantize_weight("w2_0", round_weight("w2_0", w2_raw0))
+        e_picked0 = gather_words("e0", e_table0, tok_list[:], S)
+        early_pass(w2_q0, e_picked0, e_picked_scales, E_SCALE_ROW, False)
+        w2_q1 = quantize_weight("w2_1", round_weight("w2_1", w2_raw1))
+
+        list_half = HALF // OFFSETS_PER_COLUMN
+        e_picked1 = [
+            gather_words(f"e1_{half}", e_table1, tok_list[:, half * list_half : (half + 1) * list_half], HALF)
+            for half in range(2)
+        ]
+        hidden_planes = keep.tile([P, PACK, HALF], BF16, name="hidden_planes", align_bytes=64)
+        for t in range(PACK):
+            hidden_matmul(plane_banks[t][:, :HALF], w2_q1[t], e_picked1[0][:], e_picked_scales, E_SCALE_ROW + SCALE_ROWS, slice(0, HALF), False, True)
+            nc.scalar.activation(out=hidden_planes[:, t, :], in_=plane_banks[t][:, :HALF], func=SILU)
+
+        def side_quarter(c):
+            cols = slice(HALF + c * QUARTER, HALF + (c + 1) * QUARTER)
+            passes = [
+                (w1_q0, x_picked0[:, cols], x_picked_scales, X_SCALE_ROW),
+                (w1_q1, x_picked1[:, cols], x_picked_scales, X_SCALE_ROW + SCALE_ROWS),
+                (w2_q0, e_picked0[:, cols], e_picked_scales, E_SCALE_ROW),
+                (w2_q1, e_picked1[1][:, c * QUARTER : (c + 1) * QUARTER], e_picked_scales, E_SCALE_ROW + SCALE_ROWS),
+            ]
+            for t in range(PACK):
+                for g in range(len(passes)):
+                    if t == 0 and g < len(passes) - 1:
+                        continue
+                    weight, words, scales, scale_row = passes[g]
+                    hidden_matmul(side_banks[c][:, t * QUARTER : (t + 1) * QUARTER], weight[t], words, scales, scale_row, cols, g == 0, g == len(passes) - 1)
+
+        def side_silu(c):
+            grouped = keep.tile([P, QUARTER, PACK], BF16, name=f"hidden_bf{2 + c}", align_bytes=64)
+            nc.scalar.activation(out=grouped[:], in_=side_banks[c][:].rearrange("p (t n) -> p n t", t=PACK), func=SILU)
+            return grouped
+
+        w3_pairs = [keep.tile([P, 2, P, PACK], BF16, name=f"w3_bf{u}", align_bytes=64) for u in range(2)]
+
+        def round_w3(half, copy):
+            src = w3_raw[half][:].rearrange("p j (m u e) -> p u m j e", u=2, e=2)
+            for u in range(2):
+                dst = w3_pairs[u][:, :, half * P // 2 : (half + 1) * P // 2, :].rearrange("p e m j -> p m j e")
+                copy(out=dst, in_=src[:, u])
+
+        round_w3(0, nc.vector.tensor_copy)
+        side_quarter(0)
+        side_quarter(1)
+        round_w3(1, nc.scalar.copy)
+
+        y_codes = keep.tile([P, S], U32, name="y_codes", align_bytes=64)
+        y_scales = keep.tile([P, S], U8, name="y_scales", align_bytes=64)
+        out_rows = out_0.rearrange("(p t) n -> p t n", t=PACK)
+        out_words = out_1[0].rearrange("p c r -> p (c r)").bitcast(I32)
+
+        def interleave_hidden(quarter):
+            grouped = keep.tile([P, QUARTER, PACK], BF16, name=f"hidden_bf{quarter}", align_bytes=64)
+            src = hidden_planes[:, :, quarter * QUARTER : (quarter + 1) * QUARTER]
+            nc.vector.tensor_copy(
+                out=grouped[:].rearrange("p (c i) t -> p c t i", i=4),
+                in_=src.rearrange("p t (c i) -> p c t i", i=4),
+            )
+            return grouped
+
+        def quantize_hidden(quarter, grouped):
+            return quantize(f"hidden{quarter}", grouped[:].rearrange("p n t -> p (n t)"), QUARTER)
+
+        def second_layer(quarter, hidden):
+            codes, scales = hidden
+            bank = psum.tile([P, S], F32, name=f"bank{(PACK + 2 + quarter) % 8}")
+            for t in range(PACK):
+                nc.tensor.matmul_mx(
+                    out=bank[:, t * QUARTER : (t + 1) * QUARTER],
+                    lhsT=w3_q[t][0].bitcast(FP8X4),
+                    lhsT_scale=w3_q[t][1],
+                    rhs=codes[:].bitcast(FP8X4),
+                    rhs_scale=scales[:],
+                    start=True,
+                    stop=True,
+                )
+            return bank
+
+        def add_skip(quarter, bank):
+            cols = slice(quarter * QUARTER, (quarter + 1) * QUARTER)
+            y = keep.tile([P, PACK, QUARTER], F32, name=f"y{quarter}", align_bytes=64)
+            nc.vector.tensor_tensor(
+                out=y[:], in0=bank[:].rearrange("p (t n) -> p t n", t=PACK), in1=skip_rows[quarter // 2][:, :, (quarter % 2) * QUARTER : (quarter % 2 + 1) * QUARTER], op=ADD
+            )
+            nc.sync.dma_start(out=out_rows[:, :, cols], in_=y[:])
+            grouped = keep.tile([P, QUARTER, PACK], BF16, name=f"y_bf{quarter}", align_bytes=64)
+            nc.scalar.copy(
+                out=grouped[:].rearrange("p (c i) t -> p c t i", i=4),
+                in_=y[:].rearrange("p t (c i) -> p c t i", i=4),
+            )
+            return grouped
+
+        def store_planes(quarter, grouped):
+            cols = slice(quarter * QUARTER, (quarter + 1) * QUARTER)
+            nc.vector.quantize_mx(
+                out=y_codes[:, cols].bitcast(FP8X4),
+                scales=y_scales[:, cols],
+                in_=grouped[:].rearrange("p n t -> p (n t)"),
+            )
+            nc.sync.dma_start(out=out_words[:, cols], in_=y_codes[:, cols].bitcast(I32))
+
+        h0 = interleave_hidden(0)
+        h1 = interleave_hidden(1)
+        hq0 = quantize_hidden(0, h0)
+        hq1 = quantize_hidden(1, h1)
+        w3_q = quantize_weight("w3", w3_pairs)
+        h2 = side_silu(0)
+        h3 = side_silu(1)
+        bank0 = second_layer(0, hq0)
+        bank1 = second_layer(1, hq1)
+        bank2 = second_layer(2, quantize_hidden(2, h2))
+        y0 = add_skip(0, bank0)
+        bank3 = second_layer(3, quantize_hidden(3, h3))
+        y1 = add_skip(1, bank1)
+        store_planes(0, y0)
+        y2 = add_skip(2, bank2)
+        store_planes(1, y1)
+        y3 = add_skip(3, bank3)
+        store_planes(2, y2)
+        store_planes(3, y3)
+        for q in range(P // QUADRANT):
+            engine = nc.scalar if q % 2 else nc.sync
+            engine.dma_start(
+                out=out_2[0, SCALE_ROWS * q : SCALE_ROWS * (q + 1), :].bitcast(I32),
+                in_=y_scales[QUADRANT * q : QUADRANT * q + SCALE_ROWS, :].bitcast(I32),
+            )

@@ -25,6 +25,8 @@ QUADRANT = 32
 SCALE_ROWS = 4
 X_SCALE_ROW = 0
 E_SCALE_ROW = 8
+MIDDLE = slice(QUARTER, 3 * QUARTER)
+OUTER = (slice(0, QUARTER), slice(3 * QUARTER, S))
 
 
 def tile_picked_zeagle_silu_po_kernel(
@@ -45,29 +47,32 @@ def tile_picked_zeagle_silu_po_kernel(
             nc.sync.dma_start(out=table[:], in_=words.rearrange("p c r -> p (c r)").bitcast(I32))
             return table
 
-        def clear_scales(name, scales):
+        def clear_scales(name, scales, engine):
             table = keep.tile([P, scales.shape[2]], U8, name=name + "_scale_table", align_bytes=64)
-            nc.vector.memset(table[:].bitcast(I32), 0)
+            engine.memset(table[:].bitcast(I32), 0)
             return table
 
         def load_scales(table, scales, first_row, quadrants):
             for q in quadrants:
                 top = QUADRANT * q + first_row
-                nc.sync.dma_start(
+                nc.gpsimd.dma_start(
                     out=table[top : top + 2 * SCALE_ROWS, :].bitcast(I32),
                     in_=scales[:, SCALE_ROWS * q : SCALE_ROWS * (q + 1), :].bitcast(I32),
                 )
 
-        def round_weight(name, raw):
+        def load_scale_rows(table, scales, first_row, a):
+            rows = scales[a].rearrange("(q r) c -> r q c", r=SCALE_ROWS)
+            for r in range(SCALE_ROWS):
+                top = first_row + SCALE_ROWS * a + r
+                nc.sync.dma_start(out=table[top:P:QUADRANT, :].bitcast(I32), in_=rows[r].bitcast(I32))
+
+        def round_weight(name, raw, copies):
             src = raw[:].rearrange("p j (m u e) -> p u m j e", u=2, e=2)
             pairs = []
             for u in range(2):
                 grouped = keep.tile([P, 2, P, PACK], BF16, name=f"{name}_bf{u}", align_bytes=64)
                 dst = grouped[:].rearrange("p e m j -> p m j e")
-                if u == 0:
-                    nc.vector.tensor_copy(out=dst, in_=src[:, u])
-                else:
-                    nc.scalar.copy(out=dst, in_=src[:, u])
+                copies[u](out=dst, in_=src[:, u])
                 pairs.append(grouped)
             return pairs
 
@@ -112,62 +117,66 @@ def tile_picked_zeagle_silu_po_kernel(
 
         def early_pass(weight, words, scales, scale_row, start):
             for t in range(PACK):
-                hidden_matmul(plane_banks[t][:, :HALF], weight[t], words[:, :HALF], scales, scale_row, slice(0, HALF), start, False)
+                hidden_matmul(plane_banks[t][:, :HALF], weight[t], words[:, MIDDLE], scales, scale_row, MIDDLE, start, False)
             for c in range(2):
-                cols = slice(HALF + c * QUARTER, HALF + (c + 1) * QUARTER)
+                cols = OUTER[c]
                 hidden_matmul(side_banks[c][:, :QUARTER], weight[0], words[:, cols], scales, scale_row, cols, start, False)
 
-        x_scale_table = clear_scales("x", x_scales)
-        e_scale_table = clear_scales("e", e_scales)
+        x_scale_table = clear_scales("x", x_scales, nc.gpsimd)
+        e_scale_table = clear_scales("e", e_scales, nc.vector)
+        load_scales(x_scale_table, x_scales, X_SCALE_ROW, range(P // QUADRANT))
         w1_raw0 = load_weight("w1_0", w1[:K_PASS, :])
         offs_list = keep.tile([P, S // OFFSETS_PER_COLUMN], U16, name="offs_list")
         nc.sync.dma_start(offs_list[:], offs)
-        load_scales(x_scale_table, x_scales, X_SCALE_ROW, (0, 1))
         x_table0 = load_words("x0", x_words[0])
-        load_scales(x_scale_table, x_scales, X_SCALE_ROW, (2, 3))
-        w1_raw1 = load_weight("w1_1", w1[K_PASS:, :])
         tok_list = keep.tile([P, S // OFFSETS_PER_COLUMN], U16, name="tok_list")
         nc.sync.dma_start(tok_list[:], tok)
-        load_scales(e_scale_table, e_scales, E_SCALE_ROW, (0, 1))
+        w1_raw1 = load_weight("w1_1", w1[K_PASS:, :])
+        load_scale_rows(e_scale_table, e_scales, E_SCALE_ROW, 0)
         x_table1 = load_words("x1", x_words[1])
-        load_scales(e_scale_table, e_scales, E_SCALE_ROW, (2, 3))
         w2_raw0 = load_weight("w2_0", w2[:K_PASS, :])
+        load_scale_rows(e_scale_table, e_scales, E_SCALE_ROW, 1)
         e_table0 = load_words("e0", e_words[0])
         w2_raw1 = load_weight("w2_1", w2[K_PASS:, :])
         e_table1 = load_words("e1", e_words[1])
         w3_raw = [load_weight(f"w3_{half}", w3[:, half * HALF : (half + 1) * HALF]) for half in range(2)]
         skip_rows = [load_weight(f"skip_{half}", skip[:, half * HALF : (half + 1) * HALF]) for half in range(2)]
 
-        w1_q0 = quantize_weight("w1_0", round_weight("w1_0", w1_raw0))
+        w1_q0 = quantize_weight("w1_0", round_weight("w1_0", w1_raw0, (nc.scalar.copy, nc.scalar.copy)))
         x_picked_scales = gather_scales("x", x_scale_table, offs_list[:])
         x_picked0 = gather_words("x0", x_table0, offs_list[:], S)
         early_pass(w1_q0, x_picked0, x_picked_scales, X_SCALE_ROW, True)
-        w1_q1 = quantize_weight("w1_1", round_weight("w1_1", w1_raw1))
+        w1_q1 = quantize_weight("w1_1", round_weight("w1_1", w1_raw1, (nc.scalar.copy, nc.scalar.copy)))
         x_picked1 = gather_words("x1", x_table1, offs_list[:], S)
         early_pass(w1_q1, x_picked1, x_picked_scales, X_SCALE_ROW + SCALE_ROWS, False)
         e_picked_scales = gather_scales("e", e_scale_table, tok_list[:])
-        w2_q0 = quantize_weight("w2_0", round_weight("w2_0", w2_raw0))
+        w2_q0 = quantize_weight("w2_0", round_weight("w2_0", w2_raw0, (nc.scalar.copy, nc.scalar.copy)))
         e_picked0 = gather_words("e0", e_table0, tok_list[:], S)
         early_pass(w2_q0, e_picked0, e_picked_scales, E_SCALE_ROW, False)
-        w2_q1 = quantize_weight("w2_1", round_weight("w2_1", w2_raw1))
+        w2_q1 = quantize_weight("w2_1", round_weight("w2_1", w2_raw1, (nc.vector.tensor_copy, nc.scalar.copy)))
 
-        list_half = HALF // OFFSETS_PER_COLUMN
-        e_picked1 = [
-            gather_words(f"e1_{half}", e_table1, tok_list[:, half * list_half : (half + 1) * list_half], HALF)
-            for half in range(2)
-        ]
-        hidden_planes = keep.tile([P, PACK, HALF], BF16, name="hidden_planes", align_bytes=64)
+        def gather_last(name, cols):
+            offsets = tok_list[:, cols.start // OFFSETS_PER_COLUMN : cols.stop // OFFSETS_PER_COLUMN]
+            return gather_words(name, e_table1, offsets, cols.stop - cols.start)
+
+        e_middle1 = gather_last("e1_middle", MIDDLE)
+        e_outer1 = [gather_last(f"e1_outer{c}", OUTER[c]) for c in range(2)]
+        hidden_planes = [keep.tile([P, PACK, QUARTER], BF16, name=f"hidden_planes{c}", align_bytes=64) for c in range(2)]
+
+        def plane_silu(c, t):
+            nc.scalar.activation(out=hidden_planes[c][:, t, :], in_=plane_banks[t][:, c * QUARTER : (c + 1) * QUARTER], func=SILU)
+
         for t in range(PACK):
-            hidden_matmul(plane_banks[t][:, :HALF], w2_q1[t], e_picked1[0][:], e_picked_scales, E_SCALE_ROW + SCALE_ROWS, slice(0, HALF), False, True)
-            nc.scalar.activation(out=hidden_planes[:, t, :], in_=plane_banks[t][:, :HALF], func=SILU)
+            hidden_matmul(plane_banks[t][:, :HALF], w2_q1[t], e_middle1[:], e_picked_scales, E_SCALE_ROW + SCALE_ROWS, MIDDLE, False, True)
+            plane_silu(0, t)
 
         def side_quarter(c):
-            cols = slice(HALF + c * QUARTER, HALF + (c + 1) * QUARTER)
+            cols = OUTER[c]
             passes = [
                 (w1_q0, x_picked0[:, cols], x_picked_scales, X_SCALE_ROW),
                 (w1_q1, x_picked1[:, cols], x_picked_scales, X_SCALE_ROW + SCALE_ROWS),
                 (w2_q0, e_picked0[:, cols], e_picked_scales, E_SCALE_ROW),
-                (w2_q1, e_picked1[1][:, c * QUARTER : (c + 1) * QUARTER], e_picked_scales, E_SCALE_ROW + SCALE_ROWS),
+                (w2_q1, e_outer1[c][:], e_picked_scales, E_SCALE_ROW + SCALE_ROWS),
             ]
             for t in range(PACK):
                 for g in range(len(passes)):
@@ -177,32 +186,44 @@ def tile_picked_zeagle_silu_po_kernel(
                     hidden_matmul(side_banks[c][:, t * QUARTER : (t + 1) * QUARTER], weight[t], words, scales, scale_row, cols, g == 0, g == len(passes) - 1)
 
         def side_silu(c):
-            grouped = keep.tile([P, QUARTER, PACK], BF16, name=f"hidden_bf{2 + c}", align_bytes=64)
+            grouped = keep.tile([P, QUARTER, PACK], BF16, name=f"hidden_bf{3 * c}", align_bytes=64)
             nc.scalar.activation(out=grouped[:], in_=side_banks[c][:].rearrange("p (t n) -> p n t", t=PACK), func=SILU)
             return grouped
 
-        w3_pairs = [keep.tile([P, 2, P, PACK], BF16, name=f"w3_bf{u}", align_bytes=64) for u in range(2)]
+        w3_codes = keep.tile([P, PACK, P], U32, name="w3_codes", align_bytes=64)
+        w3_scales = keep.tile([P, PACK, P], U8, name="w3_scales", align_bytes=64)
+        w3_q = [(w3_codes[:, t, :], w3_scales[:, t, :]) for t in range(PACK)]
 
-        def round_w3(half, copy):
+        def round_w3(half, u, copy):
             src = w3_raw[half][:].rearrange("p j (m u e) -> p u m j e", u=2, e=2)
-            for u in range(2):
-                dst = w3_pairs[u][:, :, half * P // 2 : (half + 1) * P // 2, :].rearrange("p e m j -> p m j e")
-                copy(out=dst, in_=src[:, u])
+            grouped = keep.tile([P, 2, P // 2, PACK], BF16, name=f"w3_bf{half}{u}", align_bytes=64)
+            copy(out=grouped[:].rearrange("p e m j -> p m j e"), in_=src[:, u])
+            return grouped
 
-        round_w3(0, nc.vector.tensor_copy)
+        def quantize_w3(half, u, grouped):
+            cols = slice(half * P // 2, (half + 1) * P // 2)
+            for e in range(2):
+                nc.vector.quantize_mx(
+                    out=w3_codes[:, 2 * u + e, cols].bitcast(FP8X4),
+                    scales=w3_scales[:, 2 * u + e, cols],
+                    in_=grouped[:, e, :, :].rearrange("p m j -> p (m j)"),
+                )
+
+        w3_first = [round_w3(0, u, nc.vector.tensor_copy) for u in range(2)]
+        for u in range(2):
+            quantize_w3(0, u, w3_first[u])
         side_quarter(0)
         side_quarter(1)
-        round_w3(1, nc.scalar.copy)
 
         y_codes = keep.tile([P, S], U32, name="y_codes", align_bytes=64)
         y_scales = keep.tile([P, S], U8, name="y_scales", align_bytes=64)
         out_rows = out_0.rearrange("(p t) n -> p t n", t=PACK)
         out_words = out_1[0].rearrange("p c r -> p (c r)").bitcast(I32)
 
-        def interleave_hidden(quarter):
+        def interleave_hidden(quarter, copy):
             grouped = keep.tile([P, QUARTER, PACK], BF16, name=f"hidden_bf{quarter}", align_bytes=64)
-            src = hidden_planes[:, :, quarter * QUARTER : (quarter + 1) * QUARTER]
-            nc.vector.tensor_copy(
+            src = hidden_planes[quarter - 1][:]
+            copy(
                 out=grouped[:].rearrange("p (c i) t -> p c t i", i=4),
                 in_=src.rearrange("p t (c i) -> p c t i", i=4),
             )
@@ -213,7 +234,7 @@ def tile_picked_zeagle_silu_po_kernel(
 
         def second_layer(quarter, hidden):
             codes, scales = hidden
-            bank = psum.tile([P, S], F32, name=f"bank{(PACK + 2 + quarter) % 8}")
+            bank = psum.tile([P, S], F32, name=f"bank{(7, 6, 0, 1)[quarter]}")
             for t in range(PACK):
                 nc.tensor.matmul_mx(
                     out=bank[:, t * QUARTER : (t + 1) * QUARTER],
@@ -234,40 +255,56 @@ def tile_picked_zeagle_silu_po_kernel(
             )
             nc.sync.dma_start(out=out_rows[:, :, cols], in_=y[:])
             grouped = keep.tile([P, QUARTER, PACK], BF16, name=f"y_bf{quarter}", align_bytes=64)
-            nc.scalar.copy(
-                out=grouped[:].rearrange("p (c i) t -> p c t i", i=4),
-                in_=y[:].rearrange("p t (c i) -> p c t i", i=4),
-            )
-            return grouped
+            return y, grouped
 
-        def store_planes(quarter, grouped):
+        def round_y(pair, copy, first, last):
+            y, grouped = pair
+            copy(
+                out=grouped[:, first:last, :].rearrange("p (c i) t -> p c t i", i=4),
+                in_=y[:, :, first:last].rearrange("p t (c i) -> p c t i", i=4),
+            )
+
+        def quantize_y(quarter, pair):
+            grouped = pair[1]
             cols = slice(quarter * QUARTER, (quarter + 1) * QUARTER)
             nc.vector.quantize_mx(
                 out=y_codes[:, cols].bitcast(FP8X4),
                 scales=y_scales[:, cols],
                 in_=grouped[:].rearrange("p n t -> p (n t)"),
             )
+
+        def store_words(half):
+            cols = slice(half * HALF, (half + 1) * HALF)
             nc.sync.dma_start(out=out_words[:, cols], in_=y_codes[:, cols].bitcast(I32))
 
-        h0 = interleave_hidden(0)
-        h1 = interleave_hidden(1)
-        hq0 = quantize_hidden(0, h0)
+        h1 = interleave_hidden(1, nc.vector.tensor_copy)
+        w3_last = [round_w3(1, 0, nc.vector.tensor_copy), round_w3(1, 1, nc.scalar.copy)]
         hq1 = quantize_hidden(1, h1)
-        w3_q = quantize_weight("w3", w3_pairs)
-        h2 = side_silu(0)
-        h3 = side_silu(1)
-        bank0 = second_layer(0, hq0)
+        for u in range(2):
+            quantize_w3(1, u, w3_last[u])
         bank1 = second_layer(1, hq1)
+        for t in range(PACK):
+            plane_silu(1, t)
+        bank0 = second_layer(0, quantize_hidden(0, side_silu(0)))
+        h2 = interleave_hidden(2, nc.scalar.copy)
+        y1 = add_skip(1, bank1)
         bank2 = second_layer(2, quantize_hidden(2, h2))
+        h3 = side_silu(1)
+        round_y(y1, nc.scalar.copy, 0, QUARTER)
         y0 = add_skip(0, bank0)
         bank3 = second_layer(3, quantize_hidden(3, h3))
-        y1 = add_skip(1, bank1)
-        store_planes(0, y0)
+        round_y(y0, nc.scalar.copy, 0, QUARTER)
+        quantize_y(1, y1)
         y2 = add_skip(2, bank2)
-        store_planes(1, y1)
+        round_y(y2, nc.scalar.copy, 0, QUARTER)
+        quantize_y(0, y0)
+        store_words(0)
         y3 = add_skip(3, bank3)
-        store_planes(2, y2)
-        store_planes(3, y3)
+        round_y(y3, nc.scalar.copy, 0, QUARTER // 2)
+        quantize_y(2, y2)
+        round_y(y3, nc.vector.tensor_copy, QUARTER // 2, QUARTER)
+        quantize_y(3, y3)
+        store_words(1)
         for q in range(P // QUADRANT):
             engine = nc.scalar if q % 2 else nc.sync
             engine.dma_start(

@@ -52,19 +52,13 @@ def tile_picked_zeagle_silu_po_kernel(
             engine.memset(table[:].bitcast(I32), 0)
             return table
 
-        def load_scales(table, scales, first_row, quadrants):
-            for q in quadrants:
-                top = QUADRANT * q + first_row
-                nc.gpsimd.dma_start(
-                    out=table[top : top + 2 * SCALE_ROWS, :].bitcast(I32),
-                    in_=scales[:, SCALE_ROWS * q : SCALE_ROWS * (q + 1), :].bitcast(I32),
+        def load_scale_rows(table, scales, first_row, rows):
+            by_row = scales.rearrange("a (q r) c -> a r q c", r=SCALE_ROWS)
+            for row in rows:
+                nc.sync.dma_start(
+                    out=table[first_row + row : P : QUADRANT, :].bitcast(I32),
+                    in_=by_row[row // SCALE_ROWS, row % SCALE_ROWS].bitcast(I32),
                 )
-
-        def load_scale_rows(table, scales, first_row, a):
-            rows = scales[a].rearrange("(q r) c -> r q c", r=SCALE_ROWS)
-            for r in range(SCALE_ROWS):
-                top = first_row + SCALE_ROWS * a + r
-                nc.sync.dma_start(out=table[top:P:QUADRANT, :].bitcast(I32), in_=rows[r].bitcast(I32))
 
         def round_weight(name, raw, copies):
             src = raw[:].rearrange("p j (m u e) -> p u m j e", u=2, e=2)
@@ -124,22 +118,26 @@ def tile_picked_zeagle_silu_po_kernel(
 
         x_scale_table = clear_scales("x", x_scales, nc.gpsimd)
         e_scale_table = clear_scales("e", e_scales, nc.vector)
-        load_scales(x_scale_table, x_scales, X_SCALE_ROW, range(P // QUADRANT))
         w1_raw0 = load_weight("w1_0", w1[:K_PASS, :])
         offs_list = keep.tile([P, S // OFFSETS_PER_COLUMN], U16, name="offs_list")
         nc.sync.dma_start(offs_list[:], offs)
-        x_table0 = load_words("x0", x_words[0])
         tok_list = keep.tile([P, S // OFFSETS_PER_COLUMN], U16, name="tok_list")
         nc.sync.dma_start(tok_list[:], tok)
+        load_scale_rows(x_scale_table, x_scales, X_SCALE_ROW, range(0, 4))
+        x_table0 = load_words("x0", x_words[0])
+        load_scale_rows(x_scale_table, x_scales, X_SCALE_ROW, range(4, 7))
         w1_raw1 = load_weight("w1_1", w1[K_PASS:, :])
-        load_scale_rows(e_scale_table, e_scales, E_SCALE_ROW, 0)
+        load_scale_rows(x_scale_table, x_scales, X_SCALE_ROW, range(7, 8))
+        load_scale_rows(e_scale_table, e_scales, E_SCALE_ROW, range(0, 2))
         x_table1 = load_words("x1", x_words[1])
+        load_scale_rows(e_scale_table, e_scales, E_SCALE_ROW, range(2, 5))
         w2_raw0 = load_weight("w2_0", w2[:K_PASS, :])
-        load_scale_rows(e_scale_table, e_scales, E_SCALE_ROW, 1)
+        load_scale_rows(e_scale_table, e_scales, E_SCALE_ROW, range(5, 8))
         e_table0 = load_words("e0", e_words[0])
         w2_raw1 = load_weight("w2_1", w2[K_PASS:, :])
+        w3_raw = [load_weight("w3_0", w3[:, :HALF])]
         e_table1 = load_words("e1", e_words[1])
-        w3_raw = [load_weight(f"w3_{half}", w3[:, half * HALF : (half + 1) * HALF]) for half in range(2)]
+        w3_raw.append(load_weight("w3_1", w3[:, HALF:]))
         skip_rows = [load_weight(f"skip_{half}", skip[:, half * HALF : (half + 1) * HALF]) for half in range(2)]
 
         w1_q0 = quantize_weight("w1_0", round_weight("w1_0", w1_raw0, (nc.scalar.copy, nc.scalar.copy)))
@@ -154,6 +152,29 @@ def tile_picked_zeagle_silu_po_kernel(
         e_picked0 = gather_words("e0", e_table0, tok_list[:], S)
         early_pass(w2_q0, e_picked0, e_picked_scales, E_SCALE_ROW, False)
         w2_q1 = quantize_weight("w2_1", round_weight("w2_1", w2_raw1, (nc.vector.tensor_copy, nc.scalar.copy)))
+
+        w3_codes = keep.tile([P, PACK, P], U32, name="w3_codes", align_bytes=64)
+        w3_scales = keep.tile([P, PACK, P], U8, name="w3_scales", align_bytes=64)
+        w3_q = [(w3_codes[:, t, :], w3_scales[:, t, :]) for t in range(PACK)]
+
+        def round_w3(half, u, copy):
+            src = w3_raw[half][:].rearrange("p j (m u e) -> p u m j e", u=2, e=2)
+            grouped = keep.tile([P, 2, P // 2, PACK], BF16, name=f"w3_bf{half}{u}", align_bytes=64)
+            copy(out=grouped[:].rearrange("p e m j -> p m j e"), in_=src[:, u])
+            return grouped
+
+        def quantize_w3(half, u, grouped):
+            cols = slice(half * P // 2, (half + 1) * P // 2)
+            for e in range(2):
+                nc.vector.quantize_mx(
+                    out=w3_codes[:, 2 * u + e, cols].bitcast(FP8X4),
+                    scales=w3_scales[:, 2 * u + e, cols],
+                    in_=grouped[:, e, :, :].rearrange("p m j -> p (m j)"),
+                )
+
+        w3_first = [round_w3(0, 0, nc.vector.tensor_copy), round_w3(0, 1, nc.scalar.copy)]
+        for u in range(2):
+            quantize_w3(0, u, w3_first[u])
 
         def gather_last(name, cols):
             offsets = tok_list[:, cols.start // OFFSETS_PER_COLUMN : cols.stop // OFFSETS_PER_COLUMN]
@@ -190,28 +211,6 @@ def tile_picked_zeagle_silu_po_kernel(
             nc.scalar.activation(out=grouped[:], in_=side_banks[c][:].rearrange("p (t n) -> p n t", t=PACK), func=SILU)
             return grouped
 
-        w3_codes = keep.tile([P, PACK, P], U32, name="w3_codes", align_bytes=64)
-        w3_scales = keep.tile([P, PACK, P], U8, name="w3_scales", align_bytes=64)
-        w3_q = [(w3_codes[:, t, :], w3_scales[:, t, :]) for t in range(PACK)]
-
-        def round_w3(half, u, copy):
-            src = w3_raw[half][:].rearrange("p j (m u e) -> p u m j e", u=2, e=2)
-            grouped = keep.tile([P, 2, P // 2, PACK], BF16, name=f"w3_bf{half}{u}", align_bytes=64)
-            copy(out=grouped[:].rearrange("p e m j -> p m j e"), in_=src[:, u])
-            return grouped
-
-        def quantize_w3(half, u, grouped):
-            cols = slice(half * P // 2, (half + 1) * P // 2)
-            for e in range(2):
-                nc.vector.quantize_mx(
-                    out=w3_codes[:, 2 * u + e, cols].bitcast(FP8X4),
-                    scales=w3_scales[:, 2 * u + e, cols],
-                    in_=grouped[:, e, :, :].rearrange("p m j -> p (m j)"),
-                )
-
-        w3_first = [round_w3(0, u, nc.vector.tensor_copy) for u in range(2)]
-        for u in range(2):
-            quantize_w3(0, u, w3_first[u])
         side_quarter(0)
         side_quarter(1)
 
@@ -277,20 +276,20 @@ def tile_picked_zeagle_silu_po_kernel(
             cols = slice(half * HALF, (half + 1) * HALF)
             nc.sync.dma_start(out=out_words[:, cols], in_=y_codes[:, cols].bitcast(I32))
 
-        h1 = interleave_hidden(1, nc.vector.tensor_copy)
         w3_last = [round_w3(1, 0, nc.vector.tensor_copy), round_w3(1, 1, nc.scalar.copy)]
-        hq1 = quantize_hidden(1, h1)
-        for u in range(2):
-            quantize_w3(1, u, w3_last[u])
+        quantize_w3(1, 0, w3_last[0])
+        hq1 = quantize_hidden(1, interleave_hidden(1, nc.vector.tensor_copy))
+        quantize_w3(1, 1, w3_last[1])
         bank1 = second_layer(1, hq1)
+        h0 = side_silu(0)
         for t in range(PACK):
             plane_silu(1, t)
-        bank0 = second_layer(0, quantize_hidden(0, side_silu(0)))
-        h2 = interleave_hidden(2, nc.scalar.copy)
         y1 = add_skip(1, bank1)
-        bank2 = second_layer(2, quantize_hidden(2, h2))
+        bank0 = second_layer(0, quantize_hidden(0, h0))
+        h2 = interleave_hidden(2, nc.vector.tensor_copy)
         h3 = side_silu(1)
         round_y(y1, nc.scalar.copy, 0, QUARTER)
+        bank2 = second_layer(2, quantize_hidden(2, h2))
         y0 = add_skip(0, bank0)
         bank3 = second_layer(3, quantize_hidden(3, h3))
         round_y(y0, nc.scalar.copy, 0, QUARTER)

from contextlib import ExitStack

import concourse.mybir as mybir

F32 = mybir.dt.float32
BF16 = mybir.dt.bfloat16
I32 = mybir.dt.int32
U32 = mybir.dt.uint32
U16 = mybir.dt.uint16
U8 = mybir.dt.uint8
FP8X4 = mybir.dt.float8_e4m3fn_x4
SILU = mybir.ActivationFunctionType.Silu
ADD = mybir.AluOpType.add

K, T, S, W, H, N = 1024, 2048, 512, 1024, 512, 512
FLOPS = 2 * (2 * K * H * S + H * N * S)

P = 128
PACK = 4
K_PASS = P * PACK
HALF = S // 2
QUARTER = S // 4
OFFSETS_PER_COLUMN = 16
QUADRANT = 32
SCALE_ROWS = 4
X_SCALE_ROW = 0
E_SCALE_ROW = 8
MIDDLE = slice(QUARTER, 3 * QUARTER)
OUTER = (slice(0, QUARTER), slice(3 * QUARTER, S))


def tile_picked_zeagle_silu_po_kernel(
    tc, x_words, x_scales, e_words, e_scales, w1, w2, w3, skip, offs, tok, out_0, out_1, out_2
):
    nc = tc.nc
    with ExitStack() as ctx:
        keep = ctx.enter_context(tc.tile_pool(name="keep", bufs=1))
        psum = ctx.enter_context(tc.psum_pool(name="psum", bufs=1))

        def load_weight(name, rows):
            raw = keep.tile([P, PACK, rows.shape[1]], F32, name=name + "_raw")
            nc.sync.dma_start(out=raw[:], in_=rows.rearrange("(p j) c -> p j c", j=PACK))
            return raw

        def load_words(name, words):
            table = keep.tile([P, words.shape[1]], I32, name=name + "_table", align_bytes=64)
            nc.sync.dma_start(out=table[:], in_=words.rearrange("p c r -> p (c r)").bitcast(I32))
            return table

        def clear_scales(name, scales, engine):
            table = keep.tile([P, scales.shape[2]], U8, name=name + "_scale_table", align_bytes=64)
            engine.memset(table[:].bitcast(I32), 0)
            return table

        def load_scale_rows(table, scales, first_row, rows):
            by_row = scales.rearrange("a (q r) c -> a r q c", r=SCALE_ROWS)
            for row in rows:
                nc.sync.dma_start(
                    out=table[first_row + row : P : QUADRANT, :].bitcast(I32),
                    in_=by_row[row // SCALE_ROWS, row % SCALE_ROWS].bitcast(I32),
                )

        def round_weight(name, raw, copies):
            src = raw[:].rearrange("p j (m u e) -> p u m j e", u=2, e=2)
            pairs = []
            for u in range(2):
                grouped = keep.tile([P, 2, P, PACK], BF16, name=f"{name}_bf{u}", align_bytes=64)
                dst = grouped[:].rearrange("p e m j -> p m j e")
                copies[u](out=dst, in_=src[:, u])
                pairs.append(grouped)
            return pairs

        def quantize(name, values, width):
            codes = keep.tile([P, width], U32, name=name + "_codes", align_bytes=64)
            scales = keep.tile([P, width], U8, name=name + "_scales", align_bytes=64)
            nc.vector.quantize_mx(out=codes[:].bitcast(FP8X4), scales=scales[:], in_=values)
            return codes, scales

        def quantize_weight(name, pairs):
            made = [
                quantize(f"{name}_q{u}", pairs[u][:].rearrange("p e m j -> p (e m j)"), 2 * P) for u in range(2)
            ]
            return [
                (made[t // 2][0][:, (t % 2) * P : (t % 2 + 1) * P], made[t // 2][1][:, (t % 2) * P : (t % 2 + 1) * P])
                for t in range(PACK)
            ]

        def gather_words(name, table, offsets, count):
            picked = keep.tile([P, count], U32, name=name + "_picked", align_bytes=64)
            nc.vector.tensor_copy(out=picked[:], in_=table[:].bitcast(U32).indirect(offsets))
            return picked

        def gather_scales(name, table, offsets):
            picked = keep.tile([P, S], U8, name=name + "_picked_scales", align_bytes=64)
            nc.vector.tensor_copy(out=picked[:], in_=table[:].indirect(offsets))
            return picked

        plane_banks = [psum.tile([P, S], F32, name=f"bank{t}") for t in range(PACK)]
        side_banks = [psum.tile([P, S], F32, name=f"bank{PACK + c}") for c in range(2)]

        def hidden_matmul(out, weight, words, scales, scale_row, cols, start, stop):
            nc.tensor.matmul_mx(
                out=out,
                lhsT=weight[0].bitcast(FP8X4),
                lhsT_scale=weight[1],
                rhs=words.bitcast(FP8X4),
                rhs_scale=scales[scale_row:, cols],
                start=start,
                stop=stop,
            )

        def early_pass(weight, words, scales, scale_row, start):
            for t in range(PACK):
                hidden_matmul(plane_banks[t][:, :HALF], weight[t], words[:, MIDDLE], scales, scale_row, MIDDLE, start, False)
            for c in range(2):
                cols = OUTER[c]
                hidden_matmul(side_banks[c][:, :QUARTER], weight[0], words[:, cols], scales, scale_row, cols, start, False)

        x_scale_table = clear_scales("x", x_scales, nc.gpsimd)
        e_scale_table = clear_scales("e", e_scales, nc.vector)
        w1_raw0 = load_weight("w1_0", w1[:K_PASS, :])
        offs_list = keep.tile([P, S // OFFSETS_PER_COLUMN], U16, name="offs_list")
        nc.sync.dma_start(offs_list[:], offs)
        tok_list = keep.tile([P, S // OFFSETS_PER_COLUMN], U16, name="tok_list")
        nc.sync.dma_start(tok_list[:], tok)
        load_scale_rows(x_scale_table, x_scales, X_SCALE_ROW, range(0, 4))
        x_table0 = load_words("x0", x_words[0])
        load_scale_rows(x_scale_table, x_scales, X_SCALE_ROW, range(4, 7))
        w1_raw1 = load_weight("w1_1", w1[K_PASS:, :])
        load_scale_rows(x_scale_table, x_scales, X_SCALE_ROW, range(7, 8))
        load_scale_rows(e_scale_table, e_scales, E_SCALE_ROW, range(0, 2))
        x_table1 = load_words("x1", x_words[1])
        load_scale_rows(e_scale_table, e_scales, E_SCALE_ROW, range(2, 5))
        w2_raw0 = load_weight("w2_0", w2[:K_PASS, :])
        load_scale_rows(e_scale_table, e_scales, E_SCALE_ROW, range(5, 8))
        e_table0 = load_words("e0", e_words[0])
        w2_raw1 = load_weight("w2_1", w2[K_PASS:, :])
        w3_raw = [load_weight("w3_0", w3[:, :HALF])]
        e_table1 = load_words("e1", e_words[1])
        w3_raw.append(load_weight("w3_1", w3[:, HALF:]))
        skip_rows = [load_weight(f"skip_{half}", skip[:, half * HALF : (half + 1) * HALF]) for half in range(2)]

        w1_q0 = quantize_weight("w1_0", round_weight("w1_0", w1_raw0, (nc.scalar.copy, nc.scalar.copy)))
        x_picked_scales = gather_scales("x", x_scale_table, offs_list[:])
        x_picked0 = gather_words("x0", x_table0, offs_list[:], S)
        early_pass(w1_q0, x_picked0, x_picked_scales, X_SCALE_ROW, True)
        w1_q1 = quantize_weight("w1_1", round_weight("w1_1", w1_raw1, (nc.scalar.copy, nc.scalar.copy)))
        x_picked1 = gather_words("x1", x_table1, offs_list[:], S)
        early_pass(w1_q1, x_picked1, x_picked_scales, X_SCALE_ROW + SCALE_ROWS, False)
        e_picked_scales = gather_scales("e", e_scale_table, tok_list[:])
        w2_q0 = quantize_weight("w2_0", round_weight("w2_0", w2_raw0, (nc.scalar.copy, nc.scalar.copy)))
        e_picked0 = gather_words("e0", e_table0, tok_list[:], S)
        early_pass(w2_q0, e_picked0, e_picked_scales, E_SCALE_ROW, False)
        w2_q1 = quantize_weight("w2_1", round_weight("w2_1", w2_raw1, (nc.vector.tensor_copy, nc.scalar.copy)))

        w3_codes = keep.tile([P, PACK, P], U32, name="w3_codes", align_bytes=64)
        w3_scales = keep.tile([P, PACK, P], U8, name="w3_scales", align_bytes=64)
        w3_q = [(w3_codes[:, t, :], w3_scales[:, t, :]) for t in range(PACK)]

        def round_w3(half, u, copy):
            src = w3_raw[half][:].rearrange("p j (m u e) -> p u m j e", u=2, e=2)
            grouped = keep.tile([P, 2, P // 2, PACK], BF16, name=f"w3_bf{half}{u}", align_bytes=64)
            copy(out=grouped[:].rearrange("p e m j -> p m j e"), in_=src[:, u])
            return grouped

        def quantize_w3(half, u, grouped):
            cols = slice(half * P // 2, (half + 1) * P // 2)
            for e in range(2):
                nc.vector.quantize_mx(
                    out=w3_codes[:, 2 * u + e, cols].bitcast(FP8X4),
                    scales=w3_scales[:, 2 * u + e, cols],
                    in_=grouped[:, e, :, :].rearrange("p m j -> p (m j)"),
                )

        w3_first = [round_w3(0, 0, nc.vector.tensor_copy), round_w3(0, 1, nc.scalar.copy)]
        for u in range(2):
            quantize_w3(0, u, w3_first[u])

        def gather_last(name, cols):
            offsets = tok_list[:, cols.start // OFFSETS_PER_COLUMN : cols.stop // OFFSETS_PER_COLUMN]
            return gather_words(name, e_table1, offsets, cols.stop - cols.start)

        e_middle1 = gather_last("e1_middle", MIDDLE)
        e_outer1 = [gather_last(f"e1_outer{c}", OUTER[c]) for c in range(2)]
        hidden_planes = [keep.tile([P, PACK, QUARTER], BF16, name=f"hidden_planes{c}", align_bytes=64) for c in range(2)]

        def plane_silu(c, t):
            nc.scalar.activation(out=hidden_planes[c][:, t, :], in_=plane_banks[t][:, c * QUARTER : (c + 1) * QUARTER], func=SILU)

        for t in range(PACK):
            hidden_matmul(plane_banks[t][:, :HALF], w2_q1[t], e_middle1[:], e_picked_scales, E_SCALE_ROW + SCALE_ROWS, MIDDLE, False, True)
            plane_silu(0, t)

        def side_quarter(c):
            cols = OUTER[c]
            passes = [
                (w1_q0, x_picked0[:, cols], x_picked_scales, X_SCALE_ROW),
                (w1_q1, x_picked1[:, cols], x_picked_scales, X_SCALE_ROW + SCALE_ROWS),
                (w2_q0, e_picked0[:, cols], e_picked_scales, E_SCALE_ROW),
                (w2_q1, e_outer1[c][:], e_picked_scales, E_SCALE_ROW + SCALE_ROWS),
            ]
            for t in range(PACK):
                for g in range(len(passes)):
                    if t == 0 and g < len(passes) - 1:
                        continue
                    weight, words, scales, scale_row = passes[g]
                    hidden_matmul(side_banks[c][:, t * QUARTER : (t + 1) * QUARTER], weight[t], words, scales, scale_row, cols, g == 0, g == len(passes) - 1)

        def side_silu(c):
            grouped = keep.tile([P, QUARTER, PACK], BF16, name=f"hidden_bf{3 * c}", align_bytes=64)
            nc.scalar.activation(out=grouped[:], in_=side_banks[c][:].rearrange("p (t n) -> p n t", t=PACK), func=SILU)
            return grouped

        side_quarter(0)
        side_quarter(1)

        y_codes = keep.tile([P, S], U32, name="y_codes", align_bytes=64)
        y_scales = keep.tile([P, S], U8, name="y_scales", align_bytes=64)
        out_rows = out_0.rearrange("(p t) n -> p t n", t=PACK)
        out_words = out_1[0].rearrange("p c r -> p (c r)").bitcast(I32)

        def interleave_hidden(quarter, copy):
            grouped = keep.tile([P, QUARTER, PACK], BF16, name=f"hidden_bf{quarter}", align_bytes=64)
            src = hidden_planes[quarter - 1][:]
            copy(
                out=grouped[:].rearrange("p (c i) t -> p c t i", i=4),
                in_=src.rearrange("p t (c i) -> p c t i", i=4),
            )
            return grouped

        def quantize_hidden(quarter, grouped):
            return quantize(f"hidden{quarter}", grouped[:].rearrange("p n t -> p (n t)"), QUARTER)

        def second_layer(quarter, hidden):
            codes, scales = hidden
            bank = psum.tile([P, S], F32, name=f"bank{(7, 6, 0, 1)[quarter]}")
            for t in range(PACK):
                nc.tensor.matmul_mx(
                    out=bank[:, t * QUARTER : (t + 1) * QUARTER],
                    lhsT=w3_q[t][0].bitcast(FP8X4),
                    lhsT_scale=w3_q[t][1],
                    rhs=codes[:].bitcast(FP8X4),
                    rhs_scale=scales[:],
                    start=True,
                    stop=True,
                )
            return bank

        def add_skip(quarter, bank):
            cols = slice(quarter * QUARTER, (quarter + 1) * QUARTER)
            y = keep.tile([P, PACK, QUARTER], F32, name=f"y{quarter}", align_bytes=64)
            nc.vector.tensor_tensor(
                out=y[:], in0=bank[:].rearrange("p (t n) -> p t n", t=PACK), in1=skip_rows[quarter // 2][:, :, (quarter % 2) * QUARTER : (quarter % 2 + 1) * QUARTER], op=ADD
            )
            nc.sync.dma_start(out=out_rows[:, :, cols], in_=y[:])
            grouped = keep.tile([P, QUARTER, PACK], BF16, name=f"y_bf{quarter}", align_bytes=64)
            return y, grouped

        def round_y(pair, copy, first, last):
            y, grouped = pair
            copy(
                out=grouped[:, first:last, :].rearrange("p (c i) t -> p c t i", i=4),
                in_=y[:, :, first:last].rearrange("p t (c i) -> p c t i", i=4),
            )

        def quantize_y(quarter, pair):
            grouped = pair[1]
            cols = slice(quarter * QUARTER, (quarter + 1) * QUARTER)
            nc.vector.quantize_mx(
                out=y_codes[:, cols].bitcast(FP8X4),
                scales=y_scales[:, cols],
                in_=grouped[:].rearrange("p n t -> p (n t)"),
            )

        def store_words(half):
            cols = slice(half * HALF, (half + 1) * HALF)
            nc.sync.dma_start(out=out_words[:, cols], in_=y_codes[:, cols].bitcast(I32))

        w3_last = [round_w3(1, 0, nc.vector.tensor_copy), round_w3(1, 1, nc.scalar.copy)]
        quantize_w3(1, 0, w3_last[0])
        hq1 = quantize_hidden(1, interleave_hidden(1, nc.vector.tensor_copy))
        quantize_w3(1, 1, w3_last[1])
        bank1 = second_layer(1, hq1)
        h0 = side_silu(0)
        for t in range(PACK):
            plane_silu(1, t)
        y1 = add_skip(1, bank1)
        bank0 = second_layer(0, quantize_hidden(0, h0))
        h2 = interleave_hidden(2, nc.vector.tensor_copy)
        h3 = side_silu(1)
        round_y(y1, nc.scalar.copy, 0, QUARTER)
        bank2 = second_layer(2, quantize_hidden(2, h2))
        y0 = add_skip(0, bank0)
        bank3 = second_layer(3, quantize_hidden(3, h3))
        round_y(y0, nc.scalar.copy, 0, QUARTER)
        quantize_y(1, y1)
        y2 = add_skip(2, bank2)
        round_y(y2, nc.scalar.copy, 0, QUARTER)
        quantize_y(0, y0)
        store_words(0)
        y3 = add_skip(3, bank3)
        round_y(y3, nc.scalar.copy, 0, QUARTER // 2)
        quantize_y(2, y2)
        round_y(y3, nc.vector.tensor_copy, QUARTER // 2, QUARTER)
        quantize_y(3, y3)
        store_words(1)
        for q in range(P // QUADRANT):
            engine = nc.scalar if q % 2 else nc.sync
            engine.dma_start(
                out=out_2[0, SCALE_ROWS * q : SCALE_ROWS * (q + 1), :].bitcast(I32),
                in_=y_scales[QUADRANT * q : QUADRANT * q + SCALE_ROWS, :].bitcast(I32),
            )
